import numpy as np
CORES = [4,132,260,388,12,140,268,396,20,148,276,404,28,156,284,412]
N = 16
def setup_inputs(rng):
    return {"x": rng.standard_normal((N, 128, 16), dtype=np.float32)}
def reference(x):
    s = np.cumsum(x.astype(np.float64), axis=0)
    return {"y": s.astype(x.dtype)}

@@ -1,0 +1,125 @@
+from concourse.bass import DstId, RemoteDMATransfer
+
+SCRATCH = {
+    "xs": ("dram", [128, 16], "float32"),
+    "src": ("dram", [4, 128, 16], "float32"),
+    "part": ("dram", [3, 128, 16], "float32"),
+    "res": ("dram", [128, 16], "float32"),
+}
+SEMAPHORES = ["loaded", "got_src", "got_part", "fin", "sent", "stored"]
+
+CAB = (3, 2, 1, 0)
+
+
+def rank_core(c, h):
+    return h * 128 + c * 8 + 4
+
+
+def hub_core(c, h):
+    return h * 128 + c * 8 + 6
+
+
+def rack_hosts(f):
+    return (0, 1) if f < 2 else (2, 3)
+
+
+def addends(k, f, c, t):
+    return tuple((cc, hh) for cc in (k % 2, k % 2 + 2) for hh in rack_hosts(f) if 4 * cc + hh <= 4 * c + t)
+
+
+def served(k, f):
+    return [(k, f), (k ^ 1, f), (k, CAB[f]), (k ^ 1, CAB[f])]
+
+
+def gathered(k, f):
+    s = set()
+    for d in served(k, f):
+        if d != (0, 0):
+            s |= set(addends(k, f, d[0], d[1]))
+    return sorted(s)
+
+
+def engines(mask):
+    return bin(mask).count("1")
+
+
+def hop2(k, f):
+    groups = {}
+    for d in served(k, f)[1:]:
+        a = addends(k, f, d[0], d[1])
+        if a:
+            groups.setdefault(a, []).append(d)
+    masks = {0: (), 1: (0xFF,), 2: (0x0F, 0xF0), 3: (0x0F, 0x30, 0xC0)}[len(groups)]
+    return [(a, ds, m) for (a, ds), m in zip(sorted(groups.items()), masks)]
+
+
+def src_slot(s):
+    return (s[0] // 2) * 2 + s[1] % 2
+
+
+def part_slot(k, f, c, t):
+    return (0 if f == t else 2) + (0 if k == c else 1) - 1 if f == t else (1 if k == c else 2)
+
+
+def rank_program(g, core, T, topo):
+    h, c, n = core // 128, (core % 128) // 8, core % 8
+    if c > 3 or n not in (4, 6):
+        return
+
+    def dst(d):
+        rid, pid = topo.addr(d, core)
+        return DstId(rid=rid, pnc=pid)
+
+    if n == 4:
+        g.sync.dma_start(T.xs[:], T.x[:]).then_inc(T.sem.loaded, 16)
+        if (c, h) == (0, 0):
+            g.scalar.dma_start(T.y[:], T.x[:]).then_inc(T.sem.stored, 16)
+        hubs = [(k, f) for f in rack_hosts(h) for k in (c % 2, c % 2 + 2) if (c, h) in gathered(k, f)]
+        slot = src_slot((c, h))
+        far = [d for d in hubs if d != (c, h)]
+        tr, sent = [], 0
+        if (c, h) in hubs:
+            tr.append(RemoteDMATransfer(dst_ids=[dst(hub_core(c, h))], dma_engine_mask=0xFF00, remote_sem=T.sem.got_src,
+                                        srcs=[T.xs[:]], dsts=[T.src[slot]], alu_op=0))
+            sent += 8
+        if far:
+            tr.append(RemoteDMATransfer(dst_ids=[dst(hub_core(k, f)) for k, f in far], dma_engine_mask=0x00FF,
+                                        remote_sem=T.sem.got_src, srcs=[T.xs[:]], dsts=[T.src[slot] for _ in far], alu_op=0))
+            sent += 8
+        g.wait_ge(T.sem.loaded, 16)
+        g.remote_dma_fused(tr, local_sem=T.sem.sent)
+        if (c, h) != (0, 0):
+            g.sync.wait_ge(T.sem.fin, 16)
+            g.sync.dma_start(T.y[:], T.res[:]).then_inc(T.sem.stored, 16)
+            g.sync.wait_ge(T.sem.stored, 16)
+        else:
+            g.scalar.wait_ge(T.sem.stored, 16)
+        g.wait_ge(T.sem.sent, sent)
+        return
+
+    k, f = c, h
+    sent = 0
+    g.wait_ge(T.sem.got_src, 8 * len(gathered(k, f)))
+    tr = []
+    for a, ds, m in hop2(k, f):
+        tr.append(RemoteDMATransfer(dst_ids=[dst(hub_core(d[0], d[1])) for d in ds], dma_engine_mask=m,
+                                    remote_sem=T.sem.got_part, srcs=[T.src[src_slot(s)] for s in a],
+                                    dsts=[T.part[part_slot(k, f, d[0], d[1])] for d in ds], alu_op=1 if len(a) > 1 else 0))
+        sent += engines(m)
+    if tr:
+        g.remote_dma_fused(tr, local_sem=T.sem.sent)
+    if (k, f) != (0, 0):
+        pieces = [T.src[src_slot(s)] for s in addends(k, f, k, f)]
+        due = 0
+        for kk, ff in served(k, f)[1:]:
+            for a, ds, m in hop2(kk, ff):
+                if (k, f) in ds:
+                    pieces.append(T.part[part_slot(kk, ff, k, f)])
+                    due += engines(m)
+        if due:
+            g.wait_ge(T.sem.got_part, due)
+        g.remote_dma_fused([RemoteDMATransfer(dst_ids=[dst(rank_core(k, f))], dma_engine_mask=0xFFFF, remote_sem=T.sem.fin,
+                                              srcs=pieces, dsts=[T.res[:]], alu_op=1 if len(pieces) > 1 else 0)],
+                           local_sem=T.sem.sent)
+        sent += 16
+    g.wait_ge(T.sem.sent, sent)

@@ -1,10 +1,13 @@
 from concourse.bass import DstId, RemoteDMATransfer
 
+HUBS = (6, 2)
+S = len(HUBS)
+W = 16 // S
 SCRATCH = {
-    "xs": ("dram", [128, 16], "float32"),
-    "src": ("dram", [4, 128, 16], "float32"),
-    "part": ("dram", [3, 128, 16], "float32"),
-    "res": ("dram", [128, 16], "float32"),
+    "xs": ("dram", [S, 128, W], "float32"),
+    "src": ("dram", [4, 128, W], "float32"),
+    "part": ("dram", [3, 128, W], "float32"),
+    "res": ("dram", [S, 128, W], "float32"),
 }
 SEMAPHORES = ["loaded", "got_src", "got_part", "fin", "sent", "stored"]
 
@@ -15,8 +18,8 @@ def rank_core(c, h):
     return h * 128 + c * 8 + 4
 
 
-def hub_core(c, h):
-    return h * 128 + c * 8 + 6
+def hub_core(c, h, q):
+    return h * 128 + c * 8 + HUBS[q]
 
 
 def rack_hosts(f):
@@ -58,18 +61,19 @@ def src_slot(s):
 
 
 def part_slot(k, f, c, t):
-    return (0 if f == t else 2) + (0 if k == c else 1) - 1 if f == t else (1 if k == c else 2)
+    return 0 if f == t else (1 if k == c else 2)
 
 
 def rank_program(g, core, T, topo):
     h, c, n = core // 128, (core % 128) // 8, core % 8
-    if c > 3 or n not in (4, 6):
+    if c > 3 or (n != 4 and n not in HUBS):
         return
 
     def dst(d):
         rid, pid = topo.addr(d, core)
         return DstId(rid=rid, pnc=pid)
 
+    E = 8 // S
     if n == 4:
         g.sync.dma_start(T.xs[:], T.x[:]).then_inc(T.sem.loaded, 16)
         if (c, h) == (0, 0):
@@ -78,14 +82,17 @@ def rank_program(g, core, T, topo):
         slot = src_slot((c, h))
         far = [d for d in hubs if d != (c, h)]
         tr, sent = [], 0
-        if (c, h) in hubs:
-            tr.append(RemoteDMATransfer(dst_ids=[dst(hub_core(c, h))], dma_engine_mask=0xFF00, remote_sem=T.sem.got_src,
-                                        srcs=[T.xs[:]], dsts=[T.src[slot]], alu_op=0))
-            sent += 8
-        if far:
-            tr.append(RemoteDMATransfer(dst_ids=[dst(hub_core(k, f)) for k, f in far], dma_engine_mask=0x00FF,
-                                        remote_sem=T.sem.got_src, srcs=[T.xs[:]], dsts=[T.src[slot] for _ in far], alu_op=0))
-            sent += 8
+        for q in range(S):
+            m = ((1 << E) - 1) << (q * E)
+            if (c, h) in hubs:
+                tr.append(RemoteDMATransfer(dst_ids=[dst(hub_core(c, h, q))], dma_engine_mask=m << 8,
+                                            remote_sem=T.sem.got_src, srcs=[T.xs[q]], dsts=[T.src[slot]], alu_op=0))
+                sent += E
+            if far:
+                tr.append(RemoteDMATransfer(dst_ids=[dst(hub_core(k, f, q)) for k, f in far], dma_engine_mask=m,
+                                            remote_sem=T.sem.got_src, srcs=[T.xs[q]], dsts=[T.src[slot] for _ in far],
+                                            alu_op=0))
+                sent += E
         g.wait_ge(T.sem.loaded, 16)
         g.remote_dma_fused(tr, local_sem=T.sem.sent)
         if (c, h) != (0, 0):
@@ -97,12 +104,12 @@ def rank_program(g, core, T, topo):
         g.wait_ge(T.sem.sent, sent)
         return
 
-    k, f = c, h
+    k, f, q = c, h, HUBS.index(n)
     sent = 0
-    g.wait_ge(T.sem.got_src, 8 * len(gathered(k, f)))
+    g.wait_ge(T.sem.got_src, E * len(gathered(k, f)))
     tr = []
     for a, ds, m in hop2(k, f):
-        tr.append(RemoteDMATransfer(dst_ids=[dst(hub_core(d[0], d[1])) for d in ds], dma_engine_mask=m,
+        tr.append(RemoteDMATransfer(dst_ids=[dst(hub_core(d[0], d[1], q)) for d in ds], dma_engine_mask=m,
                                     remote_sem=T.sem.got_part, srcs=[T.src[src_slot(s)] for s in a],
                                     dsts=[T.part[part_slot(k, f, d[0], d[1])] for d in ds], alu_op=1 if len(a) > 1 else 0))
         sent += engines(m)
@@ -118,8 +125,9 @@ def rank_program(g, core, T, topo):
                     due += engines(m)
         if due:
             g.wait_ge(T.sem.got_part, due)
-        g.remote_dma_fused([RemoteDMATransfer(dst_ids=[dst(rank_core(k, f))], dma_engine_mask=0xFFFF, remote_sem=T.sem.fin,
-                                              srcs=pieces, dsts=[T.res[:]], alu_op=1 if len(pieces) > 1 else 0)],
+        m3 = (1 << (16 // S)) - 1
+        g.remote_dma_fused([RemoteDMATransfer(dst_ids=[dst(rank_core(k, f))], dma_engine_mask=m3, remote_sem=T.sem.fin,
+                                              srcs=pieces, dsts=[T.res[q]], alu_op=1 if len(pieces) > 1 else 0)],
                            local_sem=T.sem.sent)
-        sent += 16
+        sent += 16 // S
     g.wait_ge(T.sem.sent, sent)

@@ -12,6 +12,7 @@ SCRATCH = {
 SEMAPHORES = ["loaded", "got_src", "got_part", "fin", "sent", "stored"]
 
 CAB = (3, 2, 1, 0)
+MATE = (1, 0, 3, 2)
 
 
 def rank_core(c, h):
@@ -22,16 +23,16 @@ def hub_core(c, h, q):
     return h * 128 + c * 8 + HUBS[q]
 
 
-def rack_hosts(f):
-    return (0, 1) if f < 2 else (2, 3)
+def feeders(f):
+    return (f, MATE[f])
 
 
 def addends(k, f, c, t):
-    return tuple((cc, hh) for cc in (k % 2, k % 2 + 2) for hh in rack_hosts(f) if 4 * cc + hh <= 4 * c + t)
+    return tuple(sorted((cc, hh) for cc in (k % 2, k % 2 + 2) for hh in feeders(f) if 4 * cc + hh <= 4 * c + t))
 
 
 def served(k, f):
-    return [(k, f), (k ^ 1, f), (k, CAB[f]), (k ^ 1, CAB[f])]
+    return [(k, f), (k ^ 1, CAB[f]), (k, CAB[f]), (k ^ 1, f)]
 
 
 def gathered(k, f):
@@ -78,9 +79,9 @@ def rank_program(g, core, T, topo):
         g.sync.dma_start(T.xs[:], T.x[:]).then_inc(T.sem.loaded, 16)
         if (c, h) == (0, 0):
             g.scalar.dma_start(T.y[:], T.x[:]).then_inc(T.sem.stored, 16)
-        hubs = [(k, f) for f in rack_hosts(h) for k in (c % 2, c % 2 + 2) if (c, h) in gathered(k, f)]
+        hubs = [(k, f) for f in feeders(h) for k in (c % 2, c % 2 + 2) if (c, h) in gathered(k, f)]
         slot = src_slot((c, h))
-        far = [d for d in hubs if d != (c, h)]
+        far = sorted((d for d in hubs if d != (c, h)), key=lambda d: d[0] == c)
         tr, sent = [], 0
         for q in range(S):
             m = ((1 << E) - 1) << (q * E)

@@ -1,12 +1,13 @@
 from concourse.bass import DstId, RemoteDMATransfer
 
 HUBS = (6, 2)
+LAST = (7, 3)
 S = len(HUBS)
 W = 16 // S
 SCRATCH = {
     "xs": ("dram", [S, 128, W], "float32"),
     "src": ("dram", [4, 128, W], "float32"),
-    "part": ("dram", [3, 128, W], "float32"),
+    "part": ("dram", [4, 128, W], "float32"),
     "res": ("dram", [S, 128, W], "float32"),
 }
 SEMAPHORES = ["loaded", "got_src", "got_part", "fin", "sent", "stored"]
@@ -21,6 +22,10 @@ def rank_core(c, h):
 
 def hub_core(c, h, q):
     return h * 128 + c * 8 + HUBS[q]
+
+
+def last_core(c, h, q):
+    return h * 128 + c * 8 + LAST[q]
 
 
 def feeders(f):
@@ -57,6 +62,15 @@ def hop2(k, f):
     return [(a, ds, m) for (a, ds), m in zip(sorted(groups.items()), masks)]
 
 
+def arrivals(c, t):
+    out = []
+    for kk, ff in served(c, t)[1:]:
+        for a, ds, m in hop2(kk, ff):
+            if (c, t) in ds:
+                out.append((part_slot(kk, ff, c, t), engines(m)))
+    return out
+
+
 def src_slot(s):
     return (s[0] // 2) * 2 + s[1] % 2
 
@@ -67,7 +81,7 @@ def part_slot(k, f, c, t):
 
 def rank_program(g, core, T, topo):
     h, c, n = core // 128, (core % 128) // 8, core % 8
-    if c > 3 or (n != 4 and n not in HUBS):
+    if c > 3 or (n != 4 and n not in HUBS and n not in LAST):
         return
 
     def dst(d):
@@ -97,7 +111,7 @@ def rank_program(g, core, T, topo):
         g.wait_ge(T.sem.loaded, 16)
         g.remote_dma_fused(tr, local_sem=T.sem.sent)
         if (c, h) != (0, 0):
-            g.sync.wait_ge(T.sem.fin, 16)
+            g.sync.wait_ge(T.sem.fin, S * (16 if arrivals(c, h) else 8))
             g.sync.dma_start(T.y[:], T.res[:]).then_inc(T.sem.stored, 16)
             g.sync.wait_ge(T.sem.stored, 16)
         else:
@@ -105,30 +119,37 @@ def rank_program(g, core, T, topo):
         g.wait_ge(T.sem.sent, sent)
         return
 
-    k, f, q = c, h, HUBS.index(n)
-    sent = 0
-    g.wait_ge(T.sem.got_src, E * len(gathered(k, f)))
-    tr = []
-    for a, ds, m in hop2(k, f):
-        tr.append(RemoteDMATransfer(dst_ids=[dst(hub_core(d[0], d[1], q)) for d in ds], dma_engine_mask=m,
-                                    remote_sem=T.sem.got_part, srcs=[T.src[src_slot(s)] for s in a],
-                                    dsts=[T.part[part_slot(k, f, d[0], d[1])] for d in ds], alu_op=1 if len(a) > 1 else 0))
-        sent += engines(m)
-    if tr:
+    k, f = c, h
+    if n in HUBS:
+        q = HUBS.index(n)
+        sent = 0
+        tr = []
+        for a, ds, m in hop2(k, f):
+            tr.append(RemoteDMATransfer(dst_ids=[dst(last_core(d[0], d[1], q)) for d in ds], dma_engine_mask=m,
+                                        remote_sem=T.sem.got_part, srcs=[T.src[src_slot(s)] for s in a],
+                                        dsts=[T.part[part_slot(k, f, d[0], d[1])] for d in ds],
+                                        alu_op=1 if len(a) > 1 else 0))
+            sent += engines(m)
+        if (k, f) != (0, 0):
+            a = addends(k, f, k, f)
+            if arrivals(k, f):
+                to, sem, where = last_core(k, f, q), T.sem.got_part, T.part[3]
+            else:
+                to, sem, where = rank_core(k, f), T.sem.fin, T.res[q]
+            tr.append(RemoteDMATransfer(dst_ids=[dst(to)], dma_engine_mask=0xFF00, remote_sem=sem,
+                                        srcs=[T.src[src_slot(s)] for s in a], dsts=[where], alu_op=1 if len(a) > 1 else 0))
+            sent += 8
+        g.wait_ge(T.sem.got_src, E * len(gathered(k, f)))
         g.remote_dma_fused(tr, local_sem=T.sem.sent)
-    if (k, f) != (0, 0):
-        pieces = [T.src[src_slot(s)] for s in addends(k, f, k, f)]
-        due = 0
-        for kk, ff in served(k, f)[1:]:
-            for a, ds, m in hop2(kk, ff):
-                if (k, f) in ds:
-                    pieces.append(T.part[part_slot(kk, ff, k, f)])
-                    due += engines(m)
-        if due:
-            g.wait_ge(T.sem.got_part, due)
-        m3 = (1 << (16 // S)) - 1
-        g.remote_dma_fused([RemoteDMATransfer(dst_ids=[dst(rank_core(k, f))], dma_engine_mask=m3, remote_sem=T.sem.fin,
-                                              srcs=pieces, dsts=[T.res[q]], alu_op=1 if len(pieces) > 1 else 0)],
-                           local_sem=T.sem.sent)
-        sent += 16 // S
-    g.wait_ge(T.sem.sent, sent)
+        g.wait_ge(T.sem.sent, sent)
+        return
+
+    q = LAST.index(n)
+    arr = arrivals(k, f)
+    if not arr:
+        return
+    g.wait_ge(T.sem.got_part, 8 + sum(e for _, e in arr))
+    g.remote_dma_fused([RemoteDMATransfer(dst_ids=[dst(rank_core(k, f))], dma_engine_mask=0xFFFF, remote_sem=T.sem.fin,
+                                          srcs=[T.part[3]] + [T.part[s] for s, _ in arr], dsts=[T.res[q]], alu_op=1)],
+                       local_sem=T.sem.sent)
+    g.wait_ge(T.sem.sent, 16)

from concourse.bass import DstId, RemoteDMATransfer

HUBS = (6, 2)
LAST = (7, 3)
S = len(HUBS)
W = 16 // S
SCRATCH = {
    "xs": ("dram", [S, 128, W], "float32"),
    "src": ("dram", [4, 128, W], "float32"),
    "part": ("dram", [4, 128, W], "float32"),
    "res": ("dram", [S, 128, W], "float32"),
}
SEMAPHORES = ["loaded", "got_src", "got_part", "fin", "sent", "stored"]

CAB = (3, 2, 1, 0)
MATE = (1, 0, 3, 2)


def rank_core(c, h):
    return h * 128 + c * 8 + 4


def hub_core(c, h, q):
    return h * 128 + c * 8 + HUBS[q]


def last_core(c, h, q):
    return h * 128 + c * 8 + LAST[q]


def feeders(f):
    return (f, MATE[f])


def addends(k, f, c, t):
    return tuple(sorted((cc, hh) for cc in (k % 2, k % 2 + 2) for hh in feeders(f) if 4 * cc + hh <= 4 * c + t))


def served(k, f):
    return [(k, f), (k ^ 1, CAB[f]), (k, CAB[f]), (k ^ 1, f)]


def gathered(k, f):
    s = set()
    for d in served(k, f):
        if d != (0, 0):
            s |= set(addends(k, f, d[0], d[1]))
    return sorted(s)


def engines(mask):
    return bin(mask).count("1")


def hop2(k, f):
    groups = {}
    for d in served(k, f)[1:]:
        a = addends(k, f, d[0], d[1])
        if a:
            groups.setdefault(a, []).append(d)
    masks = {0: (), 1: (0xFF,), 2: (0x0F, 0xF0), 3: (0x0F, 0x30, 0xC0)}[len(groups)]
    return [(a, ds, m) for (a, ds), m in zip(sorted(groups.items()), masks)]


def arrivals(c, t):
    out = []
    for kk, ff in served(c, t)[1:]:
        for a, ds, m in hop2(kk, ff):
            if (c, t) in ds:
                out.append((part_slot(kk, ff, c, t), engines(m)))
    return out


def src_slot(s):
    return (s[0] // 2) * 2 + s[1] % 2


def part_slot(k, f, c, t):
    return 0 if f == t else (1 if k == c else 2)


def rank_program(g, core, T, topo):
    h, c, n = core // 128, (core % 128) // 8, core % 8
    if c > 3 or (n != 4 and n not in HUBS and n not in LAST):
        return

    def dst(d):
        rid, pid = topo.addr(d, core)
        return DstId(rid=rid, pnc=pid)

    E = 8 // S
    if n == 4:
        g.sync.dma_start(T.xs[:], T.x[:]).then_inc(T.sem.loaded, 16)
        if (c, h) == (0, 0):
            g.scalar.dma_start(T.y[:], T.x[:]).then_inc(T.sem.stored, 16)
        hubs = [(k, f) for f in feeders(h) for k in (c % 2, c % 2 + 2) if (c, h) in gathered(k, f)]
        slot = src_slot((c, h))
        far = sorted((d for d in hubs if d != (c, h)), key=lambda d: d[0] == c)
        tr, sent = [], 0
        for q in range(S):
            m = ((1 << E) - 1) << (q * E)
            if (c, h) in hubs:
                tr.append(RemoteDMATransfer(dst_ids=[dst(hub_core(c, h, q))], dma_engine_mask=m << 8,
                                            remote_sem=T.sem.got_src, srcs=[T.xs[q]], dsts=[T.src[slot]], alu_op=0))
                sent += E
            if far:
                tr.append(RemoteDMATransfer(dst_ids=[dst(hub_core(k, f, q)) for k, f in far], dma_engine_mask=m,
                                            remote_sem=T.sem.got_src, srcs=[T.xs[q]], dsts=[T.src[slot] for _ in far],
                                            alu_op=0))
                sent += E
        g.wait_ge(T.sem.loaded, 16)
        g.remote_dma_fused(tr, local_sem=T.sem.sent)
        if (c, h) != (0, 0):
            g.sync.wait_ge(T.sem.fin, S * (16 if arrivals(c, h) else 8))
            g.sync.dma_start(T.y[:], T.res[:]).then_inc(T.sem.stored, 16)
            g.sync.wait_ge(T.sem.stored, 16)
        else:
            g.scalar.wait_ge(T.sem.stored, 16)
        g.wait_ge(T.sem.sent, sent)
        return

    k, f = c, h
    if n in HUBS:
        q = HUBS.index(n)
        sent = 0
        tr = []
        for a, ds, m in hop2(k, f):
            tr.append(RemoteDMATransfer(dst_ids=[dst(last_core(d[0], d[1], q)) for d in ds], dma_engine_mask=m,
                                        remote_sem=T.sem.got_part, srcs=[T.src[src_slot(s)] for s in a],
                                        dsts=[T.part[part_slot(k, f, d[0], d[1])] for d in ds],
                                        alu_op=1 if len(a) > 1 else 0))
            sent += engines(m)
        if (k, f) != (0, 0):
            a = addends(k, f, k, f)
            if arrivals(k, f):
                to, sem, where = last_core(k, f, q), T.sem.got_part, T.part[3]
            else:
                to, sem, where = rank_core(k, f), T.sem.fin, T.res[q]
            tr.append(RemoteDMATransfer(dst_ids=[dst(to)], dma_engine_mask=0xFF00, remote_sem=sem,
                                        srcs=[T.src[src_slot(s)] for s in a], dsts=[where], alu_op=1 if len(a) > 1 else 0))
            sent += 8
        g.wait_ge(T.sem.got_src, E * len(gathered(k, f)))
        g.remote_dma_fused(tr, local_sem=T.sem.sent)
        g.wait_ge(T.sem.sent, sent)
        return

    q = LAST.index(n)
    arr = arrivals(k, f)
    if not arr:
        return
    g.wait_ge(T.sem.got_part, 8 + sum(e for _, e in arr))
    g.remote_dma_fused([RemoteDMATransfer(dst_ids=[dst(rank_core(k, f))], dma_engine_mask=0xFFFF, remote_sem=T.sem.fin,
                                          srcs=[T.part[3]] + [T.part[s] for s, _ in arr], dsts=[T.res[q]], alu_op=1)],
                       local_sem=T.sem.sent)
    g.wait_ge(T.sem.sent, 16)
